import numpy as np, ml_dtypes
CORES = [9,25,41,57]
N = 4
import mx_ref
BF = ml_dtypes.bfloat16
def gentries(a):
    return np.ascontiguousarray(a.reshape(8, 16, -1).transpose(0, 2, 1)).reshape(8, -1)
def gtable(e):
    e = np.asarray(e); return np.ascontiguousarray(e.reshape(8, -1, 16).transpose(0, 2, 1)).reshape(128, -1).astype(np.int32)
def gcols(t, e):
    v = np.concatenate([t.reshape(8, 16, -1, 4), np.zeros((8, 16, 1, 4), BF)], axis=2)
    return np.ascontiguousarray(np.stack([v[g][:, e[g]] for g in range(8)])).reshape(128, -1)
def f(rng, *shape):
    return mx_ref.flush((rng.standard_normal(shape, dtype=np.float32) * np.exp2(rng.integers(-2, 3, shape[:-1] + (1,)))).astype(BF))
def wide(rng, *shape, cols=0):
    v = rng.standard_normal(shape, dtype=np.float32) * np.exp2(rng.integers(-12, 13, shape)).astype(np.float32)
    if cols: v *= np.repeat(np.exp2(rng.integers(-cols, cols + 1, shape[:-2] + (1, shape[-1] // 4))) * (rng.random(shape[:-2] + (1, shape[-1] // 4)) > 0.0625), 4, axis=-1).astype(np.float32)
    return mx_ref.flush(v.astype(BF))
S = 512
def block(rng, how):
    if how == "one": return np.full((8, S), rng.integers(0, 128))
    if how == "groups": return np.tile(rng.integers(0, 128, S), (8, 1))
    if how == "ends": return np.stack([rng.permutation(np.arange(S) % 2 * 127) for g in range(8)])
    if how == "distinct": return np.stack([np.tile(rng.permutation(128), S // 128) for g in range(8)])
    return rng.integers(0, 128, (8, S))
def lists(rng, how=""):
    return {"cw": np.stack([gtable(np.concatenate([block(rng, how) for s in range(N)], axis=1)) for r in range(N)])}
def setup_inputs(rng):
    return {"bk": f(rng, N, 128, 512), "x": f(rng, N, 128, 512 * N), **lists(rng)}
def setup_inputs_one(rng):
    return {**setup_inputs(rng), **lists(rng, "one")}
def setup_inputs_groups(rng):
    return {**setup_inputs(rng), **lists(rng, "groups")}
def setup_inputs_ends(rng):
    return {**setup_inputs(rng), **lists(rng, "ends")}
def setup_inputs_distinct(rng):
    return {**setup_inputs(rng), **lists(rng, "distinct")}
def setup_inputs_spread(rng):
    d = setup_inputs(rng); d["bk"] = wide(rng, N, 128, 512, cols=4); d["x"] = wide(rng, N, 128, 512 * N); return d
def check_inputs(d):
    b = []
    for r in range(N):
        e = d["cw"][r]
        if e.min() < 0 or e.max() > 127: b.append("cw")
    return b
def reference(bk, x, cw):
    y = np.zeros((N, 128, S), np.float32)
    for r in range(N):
        e = gentries(cw[r])
        for s in range(N):
            W = gcols(bk[s], e[:, S * s:S * s + S])
            X = np.ascontiguousarray(x[r][:, 512 * s:512 * s + 512])
            y[r] += mx_ref.matmul(mx_ref.quantize(X), mx_ref.quantize(W))
    return {"y": y}

@@ -1,0 +1,203 @@
+from concourse.bass import DstId, RemoteDMATransfer
+from concourse.mybir import dt, ActivationFunctionType
+
+N = 4
+S = 512
+H = S // 2
+CODES = "float8_e4m3fn_x4"
+LIST_ENGINES = 4
+ORDER = [
+    (0, 0, H, (256, 160, 0, 0), "own"),
+    (1, 0, H, (256, 192, 0, 0), "helper"),
+    (1, H, S, (256, 192, 0, 0), "direct"),
+    (2, 0, S, (512, 384, 0, 0), "both"),
+    (3, 0, H, (256, 192, 0, 0), "helper"),
+    (3, H, S, (256, 192, 0, 0), "direct"),
+    (0, H, S, (256, 192, 0, 0), "own"),
+]
+
+SCRATCH = {
+    "cwi": ("sbuf", [128, 128], "int32"),
+    "lst": ("sbuf", [128, 128], "uint16"),
+    "bks": ("sbuf", [128, 512], "bfloat16"),
+    "bd": ("sbuf", [128, 512], "bfloat16"),
+    "xs": ("sbuf", [128, 2048], "bfloat16"),
+    "xq": ("sbuf", [128, 512], CODES),
+    "xp": ("sbuf", [128, 512], "uint8"),
+    "yo": ("sbuf", [128, 512], "float32"),
+    "ps": ("psum", [128, 1024], "float32"),
+}
+SEMAPHORES = ["cw_in", "bk_in", "x_in", "lst_v", "bd_v", "bd_s", "x_q", "sent", "mm_a", "mm_b", "y_v", "y_s", "out_a", "out_b"]
+for _i in range(len(ORDER)):
+    SEMAPHORES += ["gv%d" % _i, "gs%d" % _i, "q%d" % _i, "hop%d" % _i]
+for _k in range(N):
+    SCRATCH["w%d" % _k] = ("sbuf", [128, 4 * S], "bfloat16")
+    SCRATCH["wq%d" % _k] = ("sbuf", [128, S], CODES)
+    SCRATCH["wp%d" % _k] = ("sbuf", [128, S], "uint8")
+    if _k:
+        SCRATCH["la%d" % _k] = ("sbuf", [128, 32], "uint16")
+        SCRATCH["aq%d" % _k] = ("sbuf", [128, S], CODES)
+        SCRATCH["ap%d" % _k] = ("sbuf", [128, S], "uint8")
+        SEMAPHORES += ["la%d" % _k, "arr%d" % _k]
+
+
+def mask_of(engines):
+    return sum(1 << e for e in engines)
+
+
+def helper_of(core, dsts, topo):
+    return [h for h in topo.cores_of(core) if topo.die(h) != topo.die(core) and all(topo.may_write(h, d) for d in dsts)][0]
+
+
+def hop_engines(src, helper, dst, topo):
+    off = topo.engines(src, dst)
+    return [e for e in topo.engines(src, helper) if e not in off]
+
+
+def handed_on(a, b, roads):
+    return {"helper": (a, b), "both": (a, (a + b) // 2)}[roads]
+
+
+def rank_program(g, core, T, topo):
+    cores = T.cores
+    sem = T.sem
+    copy = ActivationFunctionType.Copy
+
+    def codes(name, k, a, b):
+        return T["%s%d" % (name, k)][:, a:b].bitcast(dt.uint8)
+
+    def send(dst, out, in_, remote_sem, engines):
+        rid, pid, _ = topo.addr(dst)
+        g.remote_dma(out, in_, remote_sem, sem.sent, pid, rid, mask_of(engines))
+        return len(engines)
+
+    def transfer(dst, out, in_, remote_sem, engines):
+        rid, pid, _ = topo.addr(dst)
+        return RemoteDMATransfer(dst_ids=[DstId(rid=rid, pnc=pid)], dma_engine_mask=mask_of(engines), remote_sem=remote_sem, src=in_, dst=out)
+
+    helpers = [helper_of(cores[r], [c for c in cores if c != cores[r]], topo) for r in range(N)]
+    rank = T.rank_of(core)
+    if rank is None:
+        if core not in helpers:
+            return
+        r = helpers.index(core)
+        sent = 0
+        for i, (k, a, b, share, roads) in enumerate(ORDER):
+            if roads in ("helper", "both"):
+                a, b = handed_on(a, b, roads)
+                dst = cores[(r + k) % N]
+                g.wait_ge(sem["hop%d" % i], len(hop_engines(cores[r], core, dst, topo)))
+                sent += send(dst, codes("aq", k, a, b), codes("aq", k, a, b), sem["arr%d" % k], topo.engines(core, dst))
+        g.wait_ge(sem.sent, sent)
+        return
+
+    g.sync.dma_start(T.cwi[:], T.cw[:]).then_inc(sem.cw_in, 16)
+    g.scalar.dma_start(T.bks[:], T.bk[:]).then_inc(sem.bk_in, 16)
+    g.sync.dma_start(T.xs[:], T.x[:]).then_inc(sem.x_in, 16)
+
+    g.vector.wait_ge(sem.cw_in, 16)
+    g.vector.tensor_copy(T.lst[:], T.cwi[:]).then_inc(sem.lst_v, 1)
+    g.vector.wait_ge(sem.bk_in, 16)
+    for t in (0, 1):
+        g.vector.tensor_copy(T.bd[:, 128 * t:128 * t + 128], T.bks[:, t:512:4]).then_inc(sem.bd_v, 1)
+    g.scalar.wait_ge(sem.bk_in, 16)
+    for t in (2, 3):
+        g.scalar.activation(T.bd[:, 128 * t:128 * t + 128], T.bks[:, t:512:4], copy).then_inc(sem.bd_s, 1)
+    for q in (g.vector, g.scalar):
+        q.wait_ge(sem.bd_v, 2)
+        q.wait_ge(sem.bd_s, 2)
+        q.wait_ge(sem.lst_v, 1)
+
+    sent = 0
+    g.wait_ge(sem.lst_v, 1)
+    for k in range(1, N):
+        s = (rank - k) % N
+        dst = cores[s]
+        sent += send(dst, T["la%d" % k][:], T.lst[:, 32 * s:32 * s + 32], sem["la%d" % k], topo.engines(core, dst)[:LIST_ENGINES])
+
+    for i, (k, a, b, share, roads) in enumerate(ORDER):
+        r = (rank + k) % N
+        w = T["w%d" % k]
+        if k == 0:
+            off, o0 = T.lst, 32 * rank
+        else:
+            off, o0 = T["la%d" % k], 0
+            if a == 0:
+                need = len(topo.engines(cores[r], core)[:LIST_ENGINES])
+                g.vector.wait_ge(sem["la%d" % k], need)
+                g.scalar.wait_ge(sem["la%d" % k], need)
+        gv, gs, qd = sem["gv%d" % i], sem["gs%d" % i], sem["q%d" % i]
+        nv = ns = 0
+        for t in range(4):
+            m = a + share[t]
+            out = lambda u, v: w[:, 4 * u + t:4 * v:4]
+            in_ = lambda u, v: T.bd[:, 128 * t:128 * t + 128].indirect(off[:, o0 + u // 16:o0 + v // 16])
+            if m > a:
+                g.vector.tensor_copy(out(a, m), in_(a, m)).then_inc(gv, 1)
+                nv += 1
+            if m < b:
+                g.scalar.activation(out(m, b), in_(m, b), copy).then_inc(gs, 1)
+                ns += 1
+        if i == 0:
+            g.vector.wait_ge(sem.x_in, 16)
+            g.vector.quantize_mx(T.xq[:], T.xp[:], T.xs[:]).then_inc(sem.x_q, 1)
+        g.vector.wait_ge(gv, nv)
+        g.vector.wait_ge(gs, ns)
+        g.vector.quantize_mx(T["wq%d" % k][:, a:b], T["wp%d" % k][:, a:b], w[:, 4 * a:4 * b]).then_inc(qd, 1)
+        if roads == "own":
+            continue
+        dst, helper = cores[r], helpers[rank]
+        off_chip, on_chip = topo.engines(core, dst), hop_engines(core, helper, dst, topo)
+        arr, hop = sem["arr%d" % k], sem["hop%d" % i]
+        g.wait_ge(qd, 1)
+        if roads == "both":
+            c = (a + b) // 2
+            g.remote_dma_fused([transfer(helper, codes("aq", k, a, c), codes("wq", k, a, c), hop, on_chip),
+                                transfer(dst, codes("aq", k, c, b), codes("wq", k, c, b), arr, off_chip)], local_sem=sem.sent)
+            sent += len(on_chip) + len(off_chip)
+        elif roads == "helper":
+            sent += send(helper, codes("aq", k, a, b), codes("wq", k, a, b), hop, on_chip)
+        else:
+            sent += send(dst, codes("aq", k, a, b), codes("wq", k, a, b), arr, off_chip)
+        if b == S:
+            sent += send(dst, T["ap%d" % k][:], T["wp%d" % k][:], arr, off_chip)
+
+    def product(k, h, start, stop):
+        s = (rank - k) % N
+        q, p = (T["aq%d" % k], T["ap%d" % k]) if k else (T.wq0, T.wp0)
+        return g.tensor.matmul_mx(T.ps[:, 512 * h:512 * h + H], T.xq[:, 128 * s:128 * s + 128], T.xp[:, 128 * s:128 * s + 128],
+                                  q[:, H * h:H * h + H], p[:, H * h:H * h + H], start, stop)
+
+    def arrived(k):
+        s = (rank - k) % N
+        need = len(topo.engines(cores[s], core))
+        for k2, a, b, share, roads in ORDER:
+            if k2 == k:
+                need += len(topo.engines(helpers[s], core)) if roads in ("helper", "both") else 0
+                need += len(topo.engines(cores[s], core)) if roads in ("direct", "both") else 0
+        g.tensor.wait_ge(sem["arr%d" % k], need)
+
+    g.tensor.wait_ge(sem.x_q, 1)
+    g.tensor.wait_ge(sem.q0, 1)
+    product(0, 0, True, False)
+    for k in (1, 2):
+        arrived(k)
+        product(k, 0, False, False)
+        product(k, 1, k == 1, False)
+    g.tensor.wait_ge(sem["q%d" % (len(ORDER) - 1)], 1)
+    product(0, 1, False, False)
+    arrived(3)
+    product(3, 0, False, True).then_inc(sem.mm_a, 1)
+    product(3, 1, False, True).then_inc(sem.mm_b, 1)
+
+    g.vector.wait_ge(sem.mm_a, 1)
+    g.vector.tensor_copy(T.yo[:, 0:H], T.ps[:, 0:H]).then_inc(sem.y_v, 1)
+    g.sync.wait_ge(sem.y_v, 1)
+    g.sync.dma_start(T.y[:, 0:H], T.yo[:, 0:H]).then_inc(sem.out_a, 16)
+    g.sync.wait_ge(sem.out_a, 16)
+    g.scalar.wait_ge(sem.mm_b, 1)
+    g.scalar.activation(T.yo[:, H:S], T.ps[:, 512:512 + H], copy).then_inc(sem.y_s, 1)
+    g.scalar.wait_ge(sem.y_s, 1)
+    g.scalar.dma_start(T.y[:, H:S], T.yo[:, H:S]).then_inc(sem.out_b, 16)
+    g.scalar.wait_ge(sem.out_b, 16)
+    g.wait_ge(sem.sent, sent)

@@ -3,59 +3,93 @@ from concourse.mybir import dt, ActivationFunctionType
 
 N = 4
 S = 512
-H = S // 2
+U = 128
 CODES = "float8_e4m3fn_x4"
-LIST_ENGINES = 4
-ORDER = [
-    (0, 0, H, (256, 160, 0, 0), "own"),
-    (1, 0, H, (256, 192, 0, 0), "helper"),
-    (1, H, S, (256, 192, 0, 0), "direct"),
-    (2, 0, S, (512, 384, 0, 0), "both"),
-    (3, 0, H, (256, 192, 0, 0), "helper"),
-    (3, H, S, (256, 192, 0, 0), "direct"),
-    (0, H, S, (256, 192, 0, 0), "own"),
-]
+OWN = 12
+VECTOR = [("g", 0, 12, 14), ("g", 1, 12, 13), ("x",), ("q", 12, 14),
+          ("g", 0, 0, 2), ("g", 1, 0, 2), ("g", 0, 2, 4), ("q", 0, 2),
+          ("g", 0, 4, 6), ("q", 2, 4), ("g", 1, 4, 6), ("g", 0, 6, 8), ("q", 4, 6), ("g", 1, 6, 8),
+          ("g", 0, 8, 10), ("q", 6, 8), ("g", 0, 10, 12), ("q", 8, 10), ("g", 1, 11, 12), ("q", 10, 11), ("q", 11, 12),
+          ("g", 0, 14, 16), ("g", 1, 14, 16), ("q", 14, 16), ("c", 2)]
+SCALAR = [("g", 1, 13, 14), ("g", 2, 12, 14), ("g", 3, 12, 14),
+          ("g", 2, 0, 2), ("g", 3, 0, 2), ("g", 1, 2, 4), ("g", 2, 2, 4), ("g", 3, 2, 4),
+          ("g", 2, 4, 6), ("g", 3, 4, 6), ("g", 2, 6, 8), ("g", 3, 6, 8), ("g", 1, 8, 11), ("g", 2, 8, 10), ("g", 3, 8, 10),
+          ("g", 2, 10, 11), ("g", 3, 10, 11), ("g", 2, 11, 12), ("g", 3, 11, 12),
+          ("g", 2, 14, 16), ("g", 3, 14, 16), ("c", 0), ("c", 1)]
+SENDS = [[("q", 0, 2, 0)], [("p", 0, 4, 0)], [("q", 2, 4, "d")],
+         [("q", 4, 6, 0)], [("q", 6, 8, "d")], [("p", 4, 8, 0)],
+         [("q", 8, 9, 0)], [("q", 9, 11, "d")], [("q", 11, 12, 0)], [("p", 8, 12, "d")]]
+WIDE = [0, 6]
+HELPERS = [("other", 0)]
+MACHINE = 64
+LISTS = [(1, "d"), (2, "d"), (3, 0)]
+BANKS = [(0, 2), (2, 3), (3, 4)]
+PRODUCTS = [(12, 0), (0, 0), (0, 1), (0, 2), (4, 0), (4, 1), (4, 2), (12, 1), (12, 2), (8, 0), (8, 1), (8, 2)]
+STORE = ["sync", "sync", "sync"]
 
+QUANTS = [c[1:] for c in VECTOR if c[0] == "q"]
+FLAT = [t for call in SENDS for t in call]
 SCRATCH = {
     "cwi": ("sbuf", [128, 128], "int32"),
     "lst": ("sbuf", [128, 128], "uint16"),
+    "la": ("sbuf", [128, 96], "uint16"),
     "bks": ("sbuf", [128, 512], "bfloat16"),
     "bd": ("sbuf", [128, 512], "bfloat16"),
     "xs": ("sbuf", [128, 2048], "bfloat16"),
     "xq": ("sbuf", [128, 512], CODES),
     "xp": ("sbuf", [128, 512], "uint8"),
-    "yo": ("sbuf", [128, 512], "float32"),
-    "ps": ("psum", [128, 1024], "float32"),
+    "w": ("sbuf", [128, 4 * N * S], "bfloat16"),
+    "wq": ("sbuf", [128, N * S], CODES),
+    "wp": ("sbuf", [128, N * S], "uint8"),
+    "aq": ("sbuf", [128, (N - 1) * S], CODES),
+    "ap": ("sbuf", [128, (N - 1) * S], "uint8"),
+    "yo": ("sbuf", [128, S], "float32"),
+    "ps": ("psum", [128, 512 * len(BANKS)], "float32"),
 }
-SEMAPHORES = ["cw_in", "bk_in", "x_in", "lst_v", "bd_v", "bd_s", "x_q", "sent", "mm_a", "mm_b", "y_v", "y_s", "out_a", "out_b"]
-for _i in range(len(ORDER)):
-    SEMAPHORES += ["gv%d" % _i, "gs%d" % _i, "q%d" % _i, "hop%d" % _i]
-for _k in range(N):
-    SCRATCH["w%d" % _k] = ("sbuf", [128, 4 * S], "bfloat16")
-    SCRATCH["wq%d" % _k] = ("sbuf", [128, S], CODES)
-    SCRATCH["wp%d" % _k] = ("sbuf", [128, S], "uint8")
-    if _k:
-        SCRATCH["la%d" % _k] = ("sbuf", [128, 32], "uint16")
-        SCRATCH["aq%d" % _k] = ("sbuf", [128, S], CODES)
-        SCRATCH["ap%d" % _k] = ("sbuf", [128, S], "uint8")
-        SEMAPHORES += ["la%d" % _k, "arr%d" % _k]
+SEMAPHORES = ["cw_in", "bk_in", "x_in", "lst_v", "bd_v", "bd_s", "x_q", "sent"]
+SEMAPHORES += ["%s%d" % (n, i) for n in ("gv", "gs", "q") for i in range(len(QUANTS))]
+SEMAPHORES += ["hop%d" % i for i in range(len(FLAT))] + ["arr%d" % i for i in range(len(PRODUCTS))]
+SEMAPHORES += ["%s%d" % (n, k) for n in ("la", "lhop") for k in range(1, N)]
+SEMAPHORES += ["%s%d" % (n, b) for n in ("mm", "cp", "out") for b in range(len(BANKS))]
 
 
 def mask_of(engines):
     return sum(1 << e for e in engines)
 
 
-def helper_of(core, dsts, topo):
-    return [h for h in topo.cores_of(core) if topo.die(h) != topo.die(core) and all(topo.may_write(h, d) for d in dsts)][0]
+def helpers_of(core, cores, topo):
+    picked = []
+    for where, far in HELPERS:
+        near = [h for h in topo.cores_of(core) if h != core and h not in sum(picked, []) and (topo.die(h) == topo.die(core)) == (where == "same")]
+        if not far:
+            picked.append(near[:1])
+            continue
+        dst = cores[(cores.index(core) + far) % N]
+        there = [h for h in range(MACHINE) if topo.mates(topo.chip(h), topo.chip(dst)) and topo.may_write(h, dst)
+                 and h not in sum(picked, []) and topo.die(h) == topo.die(near[0])]
+        picked.append([[h for h in near if topo.may_write(h, there[0])][0], there[0]])
+    return picked
 
 
-def hop_engines(src, helper, dst, topo):
-    off = topo.engines(src, dst)
-    return [e for e in topo.engines(src, helper) if e not in off]
+def engines_of(i, off_chip, every):
+    call = SENDS[i]
+    direct = [t for t in call if t[3] == "d"]
+    hops = [t for t in call if t[3] != "d"]
+    pool = every if i in WIDE else [e for e in every if e not in off_chip]
+    out = []
+    for t in call:
+        group, es = (direct, off_chip) if t[3] == "d" else (hops, pool)
+        n = len(es) // len(group)
+        out.append(es[n * group.index(t):n * group.index(t) + n])
+    return out
 
 
-def handed_on(a, b, roads):
-    return {"helper": (a, b), "both": (a, (a + b) // 2)}[roads]
+def first_quant(a, b):
+    return [i for i, (qa, qb) in enumerate(QUANTS) if qa < b and a < qb][0]
+
+
+def first_product(a, b):
+    return [i for i, (u, bank) in enumerate(PRODUCTS) if u + BANKS[bank][0] < b and a < u + BANKS[bank][1]][0]
 
 
 def rank_program(g, core, T, topo):
@@ -63,32 +97,48 @@ def rank_program(g, core, T, topo):
     sem = T.sem
     copy = ActivationFunctionType.Copy
 
-    def codes(name, k, a, b):
-        return T["%s%d" % (name, k)][:, a:b].bitcast(dt.uint8)
+    def piece(side, what, a, b):
+        view = T[side + what][:, U * a:U * b]
+        return view.bitcast(dt.uint8) if what == "q" else view
 
-    def send(dst, out, in_, remote_sem, engines):
-        rid, pid, _ = topo.addr(dst)
-        g.remote_dma(out, in_, remote_sem, sem.sent, pid, rid, mask_of(engines))
-        return len(engines)
+    def send(transfers):
+        if len(transfers) == 1:
+            dst, out, in_, remote_sem, engines = transfers[0]
+            rid, pid, _ = topo.addr(dst)
+            g.remote_dma(out, in_, remote_sem, sem.sent, pid, rid, mask_of(engines))
+        else:
+            g.remote_dma_fused([RemoteDMATransfer(dst_ids=[DstId(rid=topo.addr(dst)[0], pnc=topo.addr(dst)[1])], dma_engine_mask=mask_of(engines),
+                                                  remote_sem=remote_sem, src=in_, dst=out)
+                                for dst, out, in_, remote_sem, engines in transfers], local_sem=sem.sent)
+        return sum(len(t[4]) for t in transfers)
 
-    def transfer(dst, out, in_, remote_sem, engines):
-        rid, pid, _ = topo.addr(dst)
-        return RemoteDMATransfer(dst_ids=[DstId(rid=rid, pnc=pid)], dma_engine_mask=mask_of(engines), remote_sem=remote_sem, src=in_, dst=out)
-
-    helpers = [helper_of(cores[r], [c for c in cores if c != cores[r]], topo) for r in range(N)]
+    helpers = [helpers_of(c, cores, topo) for c in cores]
+    off_chip = topo.engines(cores[0], cores[1])
+    every = topo.engines(cores[0], helpers[0][0][0])
+    on_chip = [e for e in every if e not in off_chip]
+    engines = sum([engines_of(i, off_chip, every) for i in range(len(SENDS))], [])
     rank = T.rank_of(core)
     if rank is None:
-        if core not in helpers:
-            return
-        r = helpers.index(core)
-        sent = 0
-        for i, (k, a, b, share, roads) in enumerate(ORDER):
-            if roads in ("helper", "both"):
-                a, b = handed_on(a, b, roads)
-                dst = cores[(r + k) % N]
-                g.wait_ge(sem["hop%d" % i], len(hop_engines(cores[r], core, dst, topo)))
-                sent += send(dst, codes("aq", k, a, b), codes("aq", k, a, b), sem["arr%d" % k], topo.engines(core, dst))
-        g.wait_ge(sem.sent, sent)
+        for r in range(N):
+            for h, chain in enumerate(helpers[r]):
+                if core not in chain:
+                    continue
+                last = core == chain[-1]
+                sent = 0
+                for k, road in LISTS:
+                    if road == h:
+                        view = T.la[:, 32 * k - 32:32 * k]
+                        g.wait_ge(sem["lhop%d" % k], len(on_chip if core == chain[0] else off_chip))
+                        sent += send([(cores[(r - k) % N] if last else chain[1], view, view, sem[("la%d" if last else "lhop%d") % k], off_chip)])
+                for i, (what, a, b, road) in enumerate(FLAT):
+                    if road == h:
+                        view = piece("a", what, a, b)
+                        g.wait_ge(sem["hop%d" % i], len(engines[i] if core == chain[0] else off_chip))
+                        if last:
+                            sent += send([(cores[(r + 1 + a // 4) % N], view, view, sem["arr%d" % first_product(a, b)], off_chip)])
+                        else:
+                            sent += send([(chain[1], view, view, sem["hop%d" % i], off_chip)])
+                g.wait_ge(sem.sent, sent)
         return
 
     g.sync.dma_start(T.cwi[:], T.cw[:]).then_inc(sem.cw_in, 16)
@@ -108,96 +158,94 @@ def rank_program(g, core, T, topo):
         q.wait_ge(sem.bd_s, 2)
         q.wait_ge(sem.lst_v, 1)
 
+    gathers = {"gv": VECTOR, "gs": SCALAR}
+    for q, name in ((g.vector, "gv"), (g.scalar, "gs")):
+        listed = set()
+        for call in gathers[name]:
+            if call[0] == "g":
+                t, a, b = call[1:]
+                if a >= OWN:
+                    off = T.lst[:, 32 * rank + 8 * (a - OWN):32 * rank + 8 * (b - OWN)]
+                else:
+                    off = T.la[:, 8 * a:8 * b]
+                    for k in range(1 + a // 4, 2 + (b - 1) // 4):
+                        if k not in listed:
+                            listed.add(k)
+                            q.wait_ge(sem["la%d" % k], len(off_chip))
+                out, in_ = T.w[:, 4 * U * a + t:4 * U * b:4], T.bd[:, 128 * t:128 * t + 128].indirect(off)
+                done = q.tensor_copy(out, in_) if name == "gv" else q.activation(out, in_, copy)
+                done.then_inc(sem["%s%d" % (name, first_quant(a, b))], 1)
+            elif call[0] == "x":
+                q.wait_ge(sem.x_in, 16)
+                q.quantize_mx(T.xq[:], T.xp[:], T.xs[:]).then_inc(sem.x_q, 1)
+            elif call[0] == "q":
+                a, b = call[1:]
+                i = QUANTS.index((a, b))
+                for other in gathers:
+                    n = len([c for c in gathers[other] if c[0] == "g" and first_quant(*c[2:]) == i])
+                    if n:
+                        q.wait_ge(sem["%s%d" % (other, i)], n)
+                q.quantize_mx(T.wq[:, U * a:U * b], T.wp[:, U * a:U * b], T.w[:, 4 * U * a:4 * U * b]).then_inc(sem["q%d" % i], 1)
+            else:
+                bank = call[1]
+                a, b = U * BANKS[bank][0], U * BANKS[bank][1]
+                q.wait_ge(sem["mm%d" % bank], 1)
+                out, in_ = T.yo[:, a:b], T.ps[:, 512 * bank:512 * bank + b - a]
+                done = q.tensor_copy(out, in_) if name == "gv" else q.activation(out, in_, copy)
+                done.then_inc(sem["cp%d" % bank], 1)
+
     sent = 0
     g.wait_ge(sem.lst_v, 1)
-    for k in range(1, N):
+    for k, road in LISTS:
         s = (rank - k) % N
-        dst = cores[s]
-        sent += send(dst, T["la%d" % k][:], T.lst[:, 32 * s:32 * s + 32], sem["la%d" % k], topo.engines(core, dst)[:LIST_ENGINES])
-
-    for i, (k, a, b, share, roads) in enumerate(ORDER):
-        r = (rank + k) % N
-        w = T["w%d" % k]
-        if k == 0:
-            off, o0 = T.lst, 32 * rank
+        out, in_ = T.la[:, 32 * k - 32:32 * k], T.lst[:, 32 * s:32 * s + 32]
+        if road == "d":
+            sent += send([(cores[s], out, in_, sem["la%d" % k], off_chip)])
         else:
-            off, o0 = T["la%d" % k], 0
-            if a == 0:
-                need = len(topo.engines(cores[r], core)[:LIST_ENGINES])
-                g.vector.wait_ge(sem["la%d" % k], need)
-                g.scalar.wait_ge(sem["la%d" % k], need)
-        gv, gs, qd = sem["gv%d" % i], sem["gs%d" % i], sem["q%d" % i]
-        nv = ns = 0
-        for t in range(4):
-            m = a + share[t]
-            out = lambda u, v: w[:, 4 * u + t:4 * v:4]
-            in_ = lambda u, v: T.bd[:, 128 * t:128 * t + 128].indirect(off[:, o0 + u // 16:o0 + v // 16])
-            if m > a:
-                g.vector.tensor_copy(out(a, m), in_(a, m)).then_inc(gv, 1)
-                nv += 1
-            if m < b:
-                g.scalar.activation(out(m, b), in_(m, b), copy).then_inc(gs, 1)
-                ns += 1
-        if i == 0:
-            g.vector.wait_ge(sem.x_in, 16)
-            g.vector.quantize_mx(T.xq[:], T.xp[:], T.xs[:]).then_inc(sem.x_q, 1)
-        g.vector.wait_ge(gv, nv)
-        g.vector.wait_ge(gs, ns)
-        g.vector.quantize_mx(T["wq%d" % k][:, a:b], T["wp%d" % k][:, a:b], w[:, 4 * a:4 * b]).then_inc(qd, 1)
-        if roads == "own":
-            continue
-        dst, helper = cores[r], helpers[rank]
-        off_chip, on_chip = topo.engines(core, dst), hop_engines(core, helper, dst, topo)
-        arr, hop = sem["arr%d" % k], sem["hop%d" % i]
-        g.wait_ge(qd, 1)
-        if roads == "both":
-            c = (a + b) // 2
-            g.remote_dma_fused([transfer(helper, codes("aq", k, a, c), codes("wq", k, a, c), hop, on_chip),
-                                transfer(dst, codes("aq", k, c, b), codes("wq", k, c, b), arr, off_chip)], local_sem=sem.sent)
-            sent += len(on_chip) + len(off_chip)
-        elif roads == "helper":
-            sent += send(helper, codes("aq", k, a, b), codes("wq", k, a, b), hop, on_chip)
-        else:
-            sent += send(dst, codes("aq", k, a, b), codes("wq", k, a, b), arr, off_chip)
-        if b == S:
-            sent += send(dst, T["ap%d" % k][:], T["wp%d" % k][:], arr, off_chip)
-
-    def product(k, h, start, stop):
-        s = (rank - k) % N
-        q, p = (T["aq%d" % k], T["ap%d" % k]) if k else (T.wq0, T.wp0)
-        return g.tensor.matmul_mx(T.ps[:, 512 * h:512 * h + H], T.xq[:, 128 * s:128 * s + 128], T.xp[:, 128 * s:128 * s + 128],
-                                  q[:, H * h:H * h + H], p[:, H * h:H * h + H], start, stop)
-
-    def arrived(k):
-        s = (rank - k) % N
-        need = len(topo.engines(cores[s], core))
-        for k2, a, b, share, roads in ORDER:
-            if k2 == k:
-                need += len(topo.engines(helpers[s], core)) if roads in ("helper", "both") else 0
-                need += len(topo.engines(cores[s], core)) if roads in ("direct", "both") else 0
-        g.tensor.wait_ge(sem["arr%d" % k], need)
+            sent += send([(helpers[rank][road][0], out, in_, sem["lhop%d" % k], on_chip)])
+    waited = set()
+    i = 0
+    for call in SENDS:
+        transfers = []
+        for what, a, b, road in call:
+            for j, (qa, qb) in enumerate(QUANTS):
+                if qa < b and a < qb and j not in waited:
+                    waited.add(j)
+                    g.wait_ge(sem["q%d" % j], 1)
+            if road == "d":
+                transfers.append((cores[(rank + 1 + a // 4) % N], piece("a", what, a, b), piece("w", what, a, b),
+                                  sem["arr%d" % first_product(a, b)], engines[i]))
+            else:
+                transfers.append((helpers[rank][road][0], piece("a", what, a, b), piece("w", what, a, b), sem["hop%d" % i], engines[i]))
+            i += 1
+        sent += send(transfers)
 
     g.tensor.wait_ge(sem.x_q, 1)
-    g.tensor.wait_ge(sem.q0, 1)
-    product(0, 0, True, False)
-    for k in (1, 2):
-        arrived(k)
-        product(k, 0, False, False)
-        product(k, 1, k == 1, False)
-    g.tensor.wait_ge(sem["q%d" % (len(ORDER) - 1)], 1)
-    product(0, 1, False, False)
-    arrived(3)
-    product(3, 0, False, True).then_inc(sem.mm_a, 1)
-    product(3, 1, False, True).then_inc(sem.mm_b, 1)
+    waited = set()
+    for i, (u, bank) in enumerate(PRODUCTS):
+        a, b = u + BANKS[bank][0], u + BANKS[bank][1]
+        if u == OWN:
+            s, side = rank, "w"
+            for j, (qa, qb) in enumerate(QUANTS):
+                if qa < b and a < qb and j not in waited:
+                    waited.add(j)
+                    g.tensor.wait_ge(sem["q%d" % j], 1)
+        else:
+            s, side = (rank - 1 - u // 4) % N, "a"
+            need = sum(len(engines[j] if t[3] == "d" else off_chip) for j, t in enumerate(FLAT) if first_product(t[1], t[2]) == i)
+            if need:
+                g.tensor.wait_ge(sem["arr%d" % i], need)
+        mine = [j for j, p in enumerate(PRODUCTS) if p[1] == bank]
+        done = g.tensor.matmul_mx(T.ps[:, 512 * bank:512 * bank + U * (b - a)], T.xq[:, 128 * s:128 * s + 128], T.xp[:, 128 * s:128 * s + 128],
+                                  T[side + "q"][:, U * a:U * b], T[side + "p"][:, U * a:U * b], i == mine[0], i == mine[-1])
+        if i == mine[-1]:
+            done.then_inc(sem["mm%d" % bank], 1)
 
-    g.vector.wait_ge(sem.mm_a, 1)
-    g.vector.tensor_copy(T.yo[:, 0:H], T.ps[:, 0:H]).then_inc(sem.y_v, 1)
-    g.sync.wait_ge(sem.y_v, 1)
-    g.sync.dma_start(T.y[:, 0:H], T.yo[:, 0:H]).then_inc(sem.out_a, 16)
-    g.sync.wait_ge(sem.out_a, 16)
-    g.scalar.wait_ge(sem.mm_b, 1)
-    g.scalar.activation(T.yo[:, H:S], T.ps[:, 512:512 + H], copy).then_inc(sem.y_s, 1)
-    g.scalar.wait_ge(sem.y_s, 1)
-    g.scalar.dma_start(T.y[:, H:S], T.yo[:, H:S]).then_inc(sem.out_b, 16)
-    g.scalar.wait_ge(sem.out_b, 16)
+    queues = {"sync": g.sync, "scalar": g.scalar}
+    for bank, (a, b) in enumerate(BANKS):
+        q = queues[STORE[bank]]
+        q.wait_ge(sem["cp%d" % bank], 1)
+        q.dma_start(T.y[:, U * a:U * b], T.yo[:, U * a:U * b]).then_inc(sem["out%d" % bank], 16)
+    for bank in range(len(BANKS)):
+        queues[STORE[bank]].wait_ge(sem["out%d" % bank], 16)
     g.wait_ge(sem.sent, sent)

@@ -6,30 +6,31 @@ S = 512
 U = 128
 CODES = "float8_e4m3fn_x4"
 OWN = 12
-VECTOR = [("g", 0, 12, 14), ("g", 1, 12, 13), ("x",), ("q", 12, 14),
-          ("g", 0, 0, 2), ("g", 1, 0, 2), ("g", 0, 2, 4), ("q", 0, 2),
-          ("g", 0, 4, 6), ("q", 2, 4), ("g", 1, 4, 6), ("g", 0, 6, 8), ("q", 4, 6), ("g", 1, 6, 8),
-          ("g", 0, 8, 10), ("q", 6, 8), ("g", 0, 10, 12), ("q", 8, 10), ("g", 1, 11, 12), ("q", 10, 11), ("q", 11, 12),
-          ("g", 0, 14, 16), ("g", 1, 14, 16), ("q", 14, 16), ("c", 2)]
+VECTOR = [("g", 0, 12, 14), ("g", 1, 12, 13), ("q", 12, 14),
+          ("g", 1, 0, 1), ("g", 0, 0, 2), ("g", 1, 1, 3), ("q", 0, 1), ("g", 0, 2, 4), ("q", 1, 2), ("g", 1, 3, 5), ("q", 2, 3),
+          ("g", 0, 4, 6), ("q", 3, 4), ("g", 0, 6, 8), ("q", 4, 5), ("q", 5, 6), ("g", 1, 7, 9), ("q", 6, 7),
+          ("g", 0, 8, 10), ("q", 7, 8), ("g", 0, 10, 12), ("q", 8, 9), ("g", 1, 10, 12), ("q", 9, 10), ("q", 10, 11), ("q", 11, 12),
+          ("x",), ("g", 0, 14, 16), ("g", 1, 14, 16), ("q", 14, 16), ("c", 1), ("c", 3)]
 SCALAR = [("g", 1, 13, 14), ("g", 2, 12, 14), ("g", 3, 12, 14),
-          ("g", 2, 0, 2), ("g", 3, 0, 2), ("g", 1, 2, 4), ("g", 2, 2, 4), ("g", 3, 2, 4),
-          ("g", 2, 4, 6), ("g", 3, 4, 6), ("g", 2, 6, 8), ("g", 3, 6, 8), ("g", 1, 8, 11), ("g", 2, 8, 10), ("g", 3, 8, 10),
-          ("g", 2, 10, 11), ("g", 3, 10, 11), ("g", 2, 11, 12), ("g", 3, 11, 12),
-          ("g", 2, 14, 16), ("g", 3, 14, 16), ("c", 0), ("c", 1)]
-SENDS = [[("q", 0, 2, 0)], [("p", 0, 4, 0)], [("q", 2, 4, "d")],
-         [("q", 4, 6, 0)], [("q", 6, 8, "d")], [("p", 4, 8, 0)],
-         [("q", 8, 9, 0)], [("q", 9, 11, "d")], [("q", 11, 12, 0)], [("p", 8, 12, "d")]]
-WIDE = [0, 6]
+          ("g", 3, 0, 1), ("g", 2, 0, 2), ("g", 3, 1, 3), ("g", 2, 2, 4), ("g", 3, 3, 5), ("g", 2, 4, 6), ("g", 1, 5, 7), ("g", 3, 5, 7),
+          ("g", 2, 6, 8), ("g", 3, 7, 9), ("g", 2, 8, 10), ("g", 1, 9, 10), ("g", 3, 9, 11), ("g", 2, 10, 12), ("g", 3, 11, 12),
+          ("g", 2, 14, 16), ("g", 3, 14, 16), ("c", 0), ("c", 2)]
+SENDS = [[("q", 0, 1, 0)], [("q", 1, 2, "d")], [("q", 2, 3, 0)], [("q", 3, 4, "d"), ("p", 0, 4, 0)],
+         [("q", 4, 5, "d")], [("q", 5, 6, 0)], [("q", 6, 7, "d")], [("q", 7, 8, 0)], [("p", 4, 8, "d")],
+         [("q", 8, 9, 0)], [("p", 8, 10, "d")], [("q", 9, 10, "d")], [("q", 10, 11, "d")], [("p", 10, 12, 0)], [("q", 11, 12, "d")]]
+WIDE = [0]
 HELPERS = [("other", 0)]
 MACHINE = 64
-LISTS = [(1, "d"), (2, "d"), (3, 0)]
-BANKS = [(0, 2), (2, 3), (3, 4)]
-PRODUCTS = [(12, 0), (0, 0), (0, 1), (0, 2), (4, 0), (4, 1), (4, 2), (12, 1), (12, 2), (8, 0), (8, 1), (8, 2)]
-STORE = ["sync", "sync", "sync"]
+LISTS = [(0, 4, "d"), (4, 8, "d"), (8, 12, 0)]
+BANKS = [(1, 2), (0, 1), (2, 3), (3, 4)]
+PRODUCTS = [(u, bank) for u in (0, 4, OWN, 8) for bank in range(len(BANKS))]
+STORE = ["sync", "sync", "sync", "sync"]
 
 QUANTS = [c[1:] for c in VECTOR if c[0] == "q"]
 FLAT = [t for call in SENDS for t in call]
 SCRATCH = {
+    "cw1": ("sbuf", [128, 32], "int32"),
+    "lst1": ("sbuf", [128, 32], "uint16"),
     "cwi": ("sbuf", [128, 128], "int32"),
     "lst": ("sbuf", [128, 128], "uint16"),
     "la": ("sbuf", [128, 96], "uint16"),
@@ -46,10 +47,10 @@ SCRATCH = {
     "yo": ("sbuf", [128, S], "float32"),
     "ps": ("psum", [128, 512 * len(BANKS)], "float32"),
 }
-SEMAPHORES = ["cw_in", "bk_in", "x_in", "lst_v", "bd_v", "bd_s", "x_q", "sent"]
+SEMAPHORES = ["cw1_in", "lst1_v", "cw_in", "bk_in", "x_in", "lst_v", "bd_v", "bd_s", "x_q", "sent"]
 SEMAPHORES += ["%s%d" % (n, i) for n in ("gv", "gs", "q") for i in range(len(QUANTS))]
 SEMAPHORES += ["hop%d" % i for i in range(len(FLAT))] + ["arr%d" % i for i in range(len(PRODUCTS))]
-SEMAPHORES += ["%s%d" % (n, k) for n in ("la", "lhop") for k in range(1, N)]
+SEMAPHORES += ["%s%d" % (n, i) for n in ("la", "lhop") for i in range(len(LISTS))]
 SEMAPHORES += ["%s%d" % (n, b) for n in ("mm", "cp", "out") for b in range(len(BANKS))]
 
 
@@ -123,33 +124,38 @@ def rank_program(g, core, T, topo):
             for h, chain in enumerate(helpers[r]):
                 if core not in chain:
                     continue
-                last = core == chain[-1]
                 sent = 0
-                for k, road in LISTS:
-                    if road == h:
-                        view = T.la[:, 32 * k - 32:32 * k]
-                        g.wait_ge(sem["lhop%d" % k], len(on_chip if core == chain[0] else off_chip))
-                        sent += send([(cores[(r - k) % N] if last else chain[1], view, view, sem[("la%d" if last else "lhop%d") % k], off_chip)])
+                for i, (a, b, road) in enumerate(LISTS):
+                    if road == h and core == chain[0]:
+                        view = T.la[:, 8 * a:8 * b]
+                        g.wait_ge(sem["lhop%d" % i], len(on_chip))
+                        sent += send([(cores[(r - 1 - a // 4) % N], view, view, sem["la%d" % i], off_chip)])
                 for i, (what, a, b, road) in enumerate(FLAT):
-                    if road == h:
+                    far = 1 + a // 4 == HELPERS[h][1]
+                    if road == h and (far or core == chain[0]):
                         view = piece("a", what, a, b)
                         g.wait_ge(sem["hop%d" % i], len(engines[i] if core == chain[0] else off_chip))
-                        if last:
+                        if core == chain[-1] or not far:
                             sent += send([(cores[(r + 1 + a // 4) % N], view, view, sem["arr%d" % first_product(a, b)], off_chip)])
                         else:
                             sent += send([(chain[1], view, view, sem["hop%d" % i], off_chip)])
                 g.wait_ge(sem.sent, sent)
         return
 
+    first = 32 * ((rank - 1) % N)
+    g.sync.dma_start(T.cw1[:], T.cw[:, first:first + 32]).then_inc(sem.cw1_in, 16)
+    g.sync.dma_start(T.bks[:], T.bk[:]).then_inc(sem.bk_in, 16)
     g.sync.dma_start(T.cwi[:], T.cw[:]).then_inc(sem.cw_in, 16)
-    g.scalar.dma_start(T.bks[:], T.bk[:]).then_inc(sem.bk_in, 16)
+    g.sync.wait_ge(sem.la0, len(off_chip))
     g.sync.dma_start(T.xs[:], T.x[:]).then_inc(sem.x_in, 16)
 
-    g.vector.wait_ge(sem.cw_in, 16)
-    g.vector.tensor_copy(T.lst[:], T.cwi[:]).then_inc(sem.lst_v, 1)
+    g.vector.wait_ge(sem.cw1_in, 16)
+    g.vector.tensor_copy(T.lst1[:], T.cw1[:]).then_inc(sem.lst1_v, 1)
     g.vector.wait_ge(sem.bk_in, 16)
     for t in (0, 1):
         g.vector.tensor_copy(T.bd[:, 128 * t:128 * t + 128], T.bks[:, t:512:4]).then_inc(sem.bd_v, 1)
+    g.vector.wait_ge(sem.cw_in, 16)
+    g.vector.tensor_copy(T.lst[:], T.cwi[:]).then_inc(sem.lst_v, 1)
     g.scalar.wait_ge(sem.bk_in, 16)
     for t in (2, 3):
         g.scalar.activation(T.bd[:, 128 * t:128 * t + 128], T.bks[:, t:512:4], copy).then_inc(sem.bd_s, 1)
@@ -168,10 +174,10 @@ def rank_program(g, core, T, topo):
                     off = T.lst[:, 32 * rank + 8 * (a - OWN):32 * rank + 8 * (b - OWN)]
                 else:
                     off = T.la[:, 8 * a:8 * b]
-                    for k in range(1 + a // 4, 2 + (b - 1) // 4):
-                        if k not in listed:
-                            listed.add(k)
-                            q.wait_ge(sem["la%d" % k], len(off_chip))
+                    for i, (la, lb, road) in enumerate(LISTS):
+                        if la < b and a < lb and i not in listed:
+                            listed.add(i)
+                            q.wait_ge(sem["la%d" % i], len(off_chip))
                 out, in_ = T.w[:, 4 * U * a + t:4 * U * b:4], T.bd[:, 128 * t:128 * t + 128].indirect(off)
                 done = q.tensor_copy(out, in_) if name == "gv" else q.activation(out, in_, copy)
                 done.then_inc(sem["%s%d" % (name, first_quant(a, b))], 1)
@@ -195,14 +201,18 @@ def rank_program(g, core, T, topo):
                 done.then_inc(sem["cp%d" % bank], 1)
 
     sent = 0
-    g.wait_ge(sem.lst_v, 1)
-    for k, road in LISTS:
-        s = (rank - k) % N
-        out, in_ = T.la[:, 32 * k - 32:32 * k], T.lst[:, 32 * s:32 * s + 32]
+    for i, (a, b, road) in enumerate(LISTS):
+        s = (rank - 1 - a // 4) % N
+        out, in_ = T.la[:, 8 * a:8 * b], T.lst[:, 32 * s + 8 * (a % 4):32 * s + 8 * (a % 4 + b - a)]
+        if i == 0:
+            g.wait_ge(sem.lst1_v, 1)
+            in_ = T.lst1[:]
+        elif i == 1:
+            g.wait_ge(sem.lst_v, 1)
         if road == "d":
-            sent += send([(cores[s], out, in_, sem["la%d" % k], off_chip)])
+            sent += send([(cores[s], out, in_, sem["la%d" % i], off_chip)])
         else:
-            sent += send([(helpers[rank][road][0], out, in_, sem["lhop%d" % k], on_chip)])
+            sent += send([(helpers[rank][road][0], out, in_, sem["lhop%d" % i], on_chip)])
     waited = set()
     i = 0
     for call in SENDS:

from concourse.bass import DstId, RemoteDMATransfer
from concourse.mybir import dt, ActivationFunctionType

N = 4
S = 512
U = 128
CODES = "float8_e4m3fn_x4"
OWN = 12
VECTOR = [("g", 0, 12, 14), ("g", 1, 12, 13), ("q", 12, 14),
          ("g", 1, 0, 1), ("g", 0, 0, 2), ("g", 1, 1, 3), ("q", 0, 1), ("g", 0, 2, 4), ("q", 1, 2), ("g", 1, 3, 5), ("q", 2, 3),
          ("g", 0, 4, 6), ("q", 3, 4), ("g", 0, 6, 8), ("q", 4, 5), ("q", 5, 6), ("g", 1, 7, 9), ("q", 6, 7),
          ("g", 0, 8, 10), ("q", 7, 8), ("g", 0, 10, 12), ("q", 8, 9), ("g", 1, 10, 12), ("q", 9, 10), ("q", 10, 11), ("q", 11, 12),
          ("x",), ("g", 0, 14, 16), ("g", 1, 14, 16), ("q", 14, 16), ("c", 1), ("c", 3)]
SCALAR = [("g", 1, 13, 14), ("g", 2, 12, 14), ("g", 3, 12, 14),
          ("g", 3, 0, 1), ("g", 2, 0, 2), ("g", 3, 1, 3), ("g", 2, 2, 4), ("g", 3, 3, 5), ("g", 2, 4, 6), ("g", 1, 5, 7), ("g", 3, 5, 7),
          ("g", 2, 6, 8), ("g", 3, 7, 9), ("g", 2, 8, 10), ("g", 1, 9, 10), ("g", 3, 9, 11), ("g", 2, 10, 12), ("g", 3, 11, 12),
          ("g", 2, 14, 16), ("g", 3, 14, 16), ("c", 0), ("c", 2)]
SENDS = [[("q", 0, 1, 0)], [("q", 1, 2, "d")], [("q", 2, 3, 0)], [("q", 3, 4, "d"), ("p", 0, 4, 0)],
         [("q", 4, 5, "d")], [("q", 5, 6, 0)], [("q", 6, 7, "d")], [("q", 7, 8, 0)], [("p", 4, 8, "d")],
         [("q", 8, 9, 0)], [("p", 8, 10, "d")], [("q", 9, 10, "d")], [("q", 10, 11, "d")], [("p", 10, 12, 0)], [("q", 11, 12, "d")]]
WIDE = [0]
HELPERS = [("other", 0)]
MACHINE = 64
LISTS = [(0, 4, "d"), (4, 8, "d"), (8, 12, 0)]
BANKS = [(1, 2), (0, 1), (2, 3), (3, 4)]
PRODUCTS = [(u, bank) for u in (0, 4, OWN, 8) for bank in range(len(BANKS))]
STORE = ["sync", "sync", "sync", "sync"]

QUANTS = [c[1:] for c in VECTOR if c[0] == "q"]
FLAT = [t for call in SENDS for t in call]
SCRATCH = {
    "cw1": ("sbuf", [128, 32], "int32"),
    "lst1": ("sbuf", [128, 32], "uint16"),
    "cwi": ("sbuf", [128, 128], "int32"),
    "lst": ("sbuf", [128, 128], "uint16"),
    "la": ("sbuf", [128, 96], "uint16"),
    "bks": ("sbuf", [128, 512], "bfloat16"),
    "bd": ("sbuf", [128, 512], "bfloat16"),
    "xs": ("sbuf", [128, 2048], "bfloat16"),
    "xq": ("sbuf", [128, 512], CODES),
    "xp": ("sbuf", [128, 512], "uint8"),
    "w": ("sbuf", [128, 4 * N * S], "bfloat16"),
    "wq": ("sbuf", [128, N * S], CODES),
    "wp": ("sbuf", [128, N * S], "uint8"),
    "aq": ("sbuf", [128, (N - 1) * S], CODES),
    "ap": ("sbuf", [128, (N - 1) * S], "uint8"),
    "yo": ("sbuf", [128, S], "float32"),
    "ps": ("psum", [128, 512 * len(BANKS)], "float32"),
}
SEMAPHORES = ["cw1_in", "lst1_v", "cw_in", "bk_in", "x_in", "lst_v", "bd_v", "bd_s", "x_q", "sent"]
SEMAPHORES += ["%s%d" % (n, i) for n in ("gv", "gs", "q") for i in range(len(QUANTS))]
SEMAPHORES += ["hop%d" % i for i in range(len(FLAT))] + ["arr%d" % i for i in range(len(PRODUCTS))]
SEMAPHORES += ["%s%d" % (n, i) for n in ("la", "lhop") for i in range(len(LISTS))]
SEMAPHORES += ["%s%d" % (n, b) for n in ("mm", "cp", "out") for b in range(len(BANKS))]


def mask_of(engines):
    return sum(1 << e for e in engines)


def helpers_of(core, cores, topo):
    picked = []
    for where, far in HELPERS:
        near = [h for h in topo.cores_of(core) if h != core and h not in sum(picked, []) and (topo.die(h) == topo.die(core)) == (where == "same")]
        if not far:
            picked.append(near[:1])
            continue
        dst = cores[(cores.index(core) + far) % N]
        there = [h for h in range(MACHINE) if topo.mates(topo.chip(h), topo.chip(dst)) and topo.may_write(h, dst)
                 and h not in sum(picked, []) and topo.die(h) == topo.die(near[0])]
        picked.append([[h for h in near if topo.may_write(h, there[0])][0], there[0]])
    return picked


def engines_of(i, off_chip, every):
    call = SENDS[i]
    direct = [t for t in call if t[3] == "d"]
    hops = [t for t in call if t[3] != "d"]
    pool = every if i in WIDE else [e for e in every if e not in off_chip]
    out = []
    for t in call:
        group, es = (direct, off_chip) if t[3] == "d" else (hops, pool)
        n = len(es) // len(group)
        out.append(es[n * group.index(t):n * group.index(t) + n])
    return out


def first_quant(a, b):
    return [i for i, (qa, qb) in enumerate(QUANTS) if qa < b and a < qb][0]


def first_product(a, b):
    return [i for i, (u, bank) in enumerate(PRODUCTS) if u + BANKS[bank][0] < b and a < u + BANKS[bank][1]][0]


def rank_program(g, core, T, topo):
    cores = T.cores
    sem = T.sem
    copy = ActivationFunctionType.Copy

    def piece(side, what, a, b):
        view = T[side + what][:, U * a:U * b]
        return view.bitcast(dt.uint8) if what == "q" else view

    def send(transfers):
        if len(transfers) == 1:
            dst, out, in_, remote_sem, engines = transfers[0]
            rid, pid, _ = topo.addr(dst)
            g.remote_dma(out, in_, remote_sem, sem.sent, pid, rid, mask_of(engines))
        else:
            g.remote_dma_fused([RemoteDMATransfer(dst_ids=[DstId(rid=topo.addr(dst)[0], pnc=topo.addr(dst)[1])], dma_engine_mask=mask_of(engines),
                                                  remote_sem=remote_sem, src=in_, dst=out)
                                for dst, out, in_, remote_sem, engines in transfers], local_sem=sem.sent)
        return sum(len(t[4]) for t in transfers)

    helpers = [helpers_of(c, cores, topo) for c in cores]
    off_chip = topo.engines(cores[0], cores[1])
    every = topo.engines(cores[0], helpers[0][0][0])
    on_chip = [e for e in every if e not in off_chip]
    engines = sum([engines_of(i, off_chip, every) for i in range(len(SENDS))], [])
    rank = T.rank_of(core)
    if rank is None:
        for r in range(N):
            for h, chain in enumerate(helpers[r]):
                if core not in chain:
                    continue
                sent = 0
                for i, (a, b, road) in enumerate(LISTS):
                    if road == h and core == chain[0]:
                        view = T.la[:, 8 * a:8 * b]
                        g.wait_ge(sem["lhop%d" % i], len(on_chip))
                        sent += send([(cores[(r - 1 - a // 4) % N], view, view, sem["la%d" % i], off_chip)])
                for i, (what, a, b, road) in enumerate(FLAT):
                    far = 1 + a // 4 == HELPERS[h][1]
                    if road == h and (far or core == chain[0]):
                        view = piece("a", what, a, b)
                        g.wait_ge(sem["hop%d" % i], len(engines[i] if core == chain[0] else off_chip))
                        if core == chain[-1] or not far:
                            sent += send([(cores[(r + 1 + a // 4) % N], view, view, sem["arr%d" % first_product(a, b)], off_chip)])
                        else:
                            sent += send([(chain[1], view, view, sem["hop%d" % i], off_chip)])
                g.wait_ge(sem.sent, sent)
        return

    first = 32 * ((rank - 1) % N)
    g.sync.dma_start(T.cw1[:], T.cw[:, first:first + 32]).then_inc(sem.cw1_in, 16)
    g.sync.dma_start(T.bks[:], T.bk[:]).then_inc(sem.bk_in, 16)
    g.sync.dma_start(T.cwi[:], T.cw[:]).then_inc(sem.cw_in, 16)
    g.sync.wait_ge(sem.la0, len(off_chip))
    g.sync.dma_start(T.xs[:], T.x[:]).then_inc(sem.x_in, 16)

    g.vector.wait_ge(sem.cw1_in, 16)
    g.vector.tensor_copy(T.lst1[:], T.cw1[:]).then_inc(sem.lst1_v, 1)
    g.vector.wait_ge(sem.bk_in, 16)
    for t in (0, 1):
        g.vector.tensor_copy(T.bd[:, 128 * t:128 * t + 128], T.bks[:, t:512:4]).then_inc(sem.bd_v, 1)
    g.vector.wait_ge(sem.cw_in, 16)
    g.vector.tensor_copy(T.lst[:], T.cwi[:]).then_inc(sem.lst_v, 1)
    g.scalar.wait_ge(sem.bk_in, 16)
    for t in (2, 3):
        g.scalar.activation(T.bd[:, 128 * t:128 * t + 128], T.bks[:, t:512:4], copy).then_inc(sem.bd_s, 1)
    for q in (g.vector, g.scalar):
        q.wait_ge(sem.bd_v, 2)
        q.wait_ge(sem.bd_s, 2)
        q.wait_ge(sem.lst_v, 1)

    gathers = {"gv": VECTOR, "gs": SCALAR}
    for q, name in ((g.vector, "gv"), (g.scalar, "gs")):
        listed = set()
        for call in gathers[name]:
            if call[0] == "g":
                t, a, b = call[1:]
                if a >= OWN:
                    off = T.lst[:, 32 * rank + 8 * (a - OWN):32 * rank + 8 * (b - OWN)]
                else:
                    off = T.la[:, 8 * a:8 * b]
                    for i, (la, lb, road) in enumerate(LISTS):
                        if la < b and a < lb and i not in listed:
                            listed.add(i)
                            q.wait_ge(sem["la%d" % i], len(off_chip))
                out, in_ = T.w[:, 4 * U * a + t:4 * U * b:4], T.bd[:, 128 * t:128 * t + 128].indirect(off)
                done = q.tensor_copy(out, in_) if name == "gv" else q.activation(out, in_, copy)
                done.then_inc(sem["%s%d" % (name, first_quant(a, b))], 1)
            elif call[0] == "x":
                q.wait_ge(sem.x_in, 16)
                q.quantize_mx(T.xq[:], T.xp[:], T.xs[:]).then_inc(sem.x_q, 1)
            elif call[0] == "q":
                a, b = call[1:]
                i = QUANTS.index((a, b))
                for other in gathers:
                    n = len([c for c in gathers[other] if c[0] == "g" and first_quant(*c[2:]) == i])
                    if n:
                        q.wait_ge(sem["%s%d" % (other, i)], n)
                q.quantize_mx(T.wq[:, U * a:U * b], T.wp[:, U * a:U * b], T.w[:, 4 * U * a:4 * U * b]).then_inc(sem["q%d" % i], 1)
            else:
                bank = call[1]
                a, b = U * BANKS[bank][0], U * BANKS[bank][1]
                q.wait_ge(sem["mm%d" % bank], 1)
                out, in_ = T.yo[:, a:b], T.ps[:, 512 * bank:512 * bank + b - a]
                done = q.tensor_copy(out, in_) if name == "gv" else q.activation(out, in_, copy)
                done.then_inc(sem["cp%d" % bank], 1)

    sent = 0
    for i, (a, b, road) in enumerate(LISTS):
        s = (rank - 1 - a // 4) % N
        out, in_ = T.la[:, 8 * a:8 * b], T.lst[:, 32 * s + 8 * (a % 4):32 * s + 8 * (a % 4 + b - a)]
        if i == 0:
            g.wait_ge(sem.lst1_v, 1)
            in_ = T.lst1[:]
        elif i == 1:
            g.wait_ge(sem.lst_v, 1)
        if road == "d":
            sent += send([(cores[s], out, in_, sem["la%d" % i], off_chip)])
        else:
            sent += send([(helpers[rank][road][0], out, in_, sem["lhop%d" % i], on_chip)])
    waited = set()
    i = 0
    for call in SENDS:
        transfers = []
        for what, a, b, road in call:
            for j, (qa, qb) in enumerate(QUANTS):
                if qa < b and a < qb and j not in waited:
                    waited.add(j)
                    g.wait_ge(sem["q%d" % j], 1)
            if road == "d":
                transfers.append((cores[(rank + 1 + a // 4) % N], piece("a", what, a, b), piece("w", what, a, b),
                                  sem["arr%d" % first_product(a, b)], engines[i]))
            else:
                transfers.append((helpers[rank][road][0], piece("a", what, a, b), piece("w", what, a, b), sem["hop%d" % i], engines[i]))
            i += 1
        sent += send(transfers)

    g.tensor.wait_ge(sem.x_q, 1)
    waited = set()
    for i, (u, bank) in enumerate(PRODUCTS):
        a, b = u + BANKS[bank][0], u + BANKS[bank][1]
        if u == OWN:
            s, side = rank, "w"
            for j, (qa, qb) in enumerate(QUANTS):
                if qa < b and a < qb and j not in waited:
                    waited.add(j)
                    g.tensor.wait_ge(sem["q%d" % j], 1)
        else:
            s, side = (rank - 1 - u // 4) % N, "a"
            need = sum(len(engines[j] if t[3] == "d" else off_chip) for j, t in enumerate(FLAT) if first_product(t[1], t[2]) == i)
            if need:
                g.tensor.wait_ge(sem["arr%d" % i], need)
        mine = [j for j, p in enumerate(PRODUCTS) if p[1] == bank]
        done = g.tensor.matmul_mx(T.ps[:, 512 * bank:512 * bank + U * (b - a)], T.xq[:, 128 * s:128 * s + 128], T.xp[:, 128 * s:128 * s + 128],
                                  T[side + "q"][:, U * a:U * b], T[side + "p"][:, U * a:U * b], i == mine[0], i == mine[-1])
        if i == mine[-1]:
            done.then_inc(sem["mm%d" % bank], 1)

    queues = {"sync": g.sync, "scalar": g.scalar}
    for bank, (a, b) in enumerate(BANKS):
        q = queues[STORE[bank]]
        q.wait_ge(sem["cp%d" % bank], 1)
        q.dma_start(T.y[:, U * a:U * b], T.yo[:, U * a:U * b]).then_inc(sem["out%d" % bank], 16)
    for bank in range(len(BANKS)):
        queues[STORE[bank]].wait_ge(sem["out%d" % bank], 16)
    g.wait_ge(sem.sent, sent)
